import numpy as np
import ml_dtypes


def mxq(x, axis, fmt="e4m3"):
    dtype, down = {"e4m3": (ml_dtypes.float8_e4m3fn, 7), "e5m2": (ml_dtypes.float8_e5m2, 14)}[fmt]
    v = np.moveaxis(np.asarray(x, np.float32).astype(ml_dtypes.bfloat16).astype(np.float64), axis, -1)
    blocks = v.reshape(v.shape[:-1] + (-1, 32))
    amax = np.abs(blocks).max(-1, keepdims=True)
    byte = np.maximum(np.where(amax > 0, np.frexp(amax)[1] - 1 + 127, 0) - down, 1)
    scale = np.exp2(byte - 127.0)
    codes = (blocks / scale).astype(np.float32).astype(dtype).astype(np.float64)
    return np.moveaxis((codes * scale).reshape(v.shape), -1, axis)


WIDE = False


def mx_kscale(k):
    if not WIDE:
        return np.ones(k)
    levels = np.array([10, -10, 5, -5, 0])
    if k % 512:
        return np.exp2(np.random.permutation(np.resize(levels, k // 32))).repeat(32)
    a = np.empty((k // 512, 16))
    for p in range(k // 512):
        a[p, :8] = np.random.permutation(np.resize(levels, 8))
        for g in range(8):
            far = levels[np.abs(levels - a[p, g]) >= 10]
            a[p, g + 8] = far[np.random.randint(len(far))]
    return np.exp2(a.ravel()).repeat(32)


BF16 = ml_dtypes.bfloat16


def bf(x):
    return np.asarray(x, np.float32).astype(BF16)


def f64(x):
    return np.asarray(x).astype(np.float64)


E2M1 = np.array([0.0, 0.5, 1.0, 1.5, 2.0, 3.0, 4.0, 6.0, -0.0, -0.5, -1.0, -1.5, -2.0, -3.0, -4.0, -6.0])


def pack_weight(w, fmt):
    k, n = w.shape
    w = f64(bf(w)).reshape(k // 32, 32, n)
    amax = np.abs(w).max(1)
    if fmt == "e4m3":
        byte = np.frexp(amax)[1] - 1 + 127 - 7
    else:
        mant, ex = np.frexp(amax / 6.0)
        byte = np.where(mant > 0.5, ex, ex - 1) + 127
    byte = np.clip(np.where(amax > 0, byte, 1), 1, 254)
    scaled = (w * np.exp2(127.0 - byte)[:, None, :]).reshape(k, n).astype(np.float32)
    by_word = np.ascontiguousarray(scaled.reshape(k // 512, 128, 4, n).transpose(0, 1, 3, 2))
    if fmt == "e4m3":
        words = by_word.astype(ml_dtypes.float8_e4m3fn).view(np.uint8)
    else:
        c = by_word.astype(ml_dtypes.float4_e2m1fn).view(np.uint8) & 0xF
        words = c[..., 0::2] | (c[..., 1::2] << 4)
    return np.ascontiguousarray(words), np.ascontiguousarray(byte.astype(np.uint8).reshape(k // 512, 16, n))


def unpack_weight(words, scales, fmt):
    g, p, n, _ = words.shape
    if fmt == "e4m3":
        vals = np.ascontiguousarray(words).view(ml_dtypes.float8_e4m3fn).astype(np.float64)
    else:
        nib = np.empty((g, p, n, 4), np.uint8)
        nib[..., 0::2] = words & 0xF
        nib[..., 1::2] = words >> 4
        vals = E2M1[nib]
    vals = vals * np.repeat(np.exp2(scales.astype(np.float64) - 127.0), 8, axis=1)[..., None]
    return vals.transpose(0, 1, 3, 2).reshape(g * 512, n)
def pack4(w):
    words, scales = pack_weight(w, "e2m1")
    return words.reshape(words.shape[0], 128, -1), scales


def unpack4(words, scales):
    return unpack_weight(words.reshape(words.shape[0], 128, -1, 2), scales, "e2m1")


G, M, K, F, N = 4, 512, 1024, 512, 1024


def setup_inputs():
    s = mx_kscale(G * K).reshape(G, K)
    t = mx_kscale(G * F).reshape(G, F)
    re = np.random.standard_normal((G, M, K)) * s[:, None, :]
    im = np.random.standard_normal((G, M, K)) * s[:, None, :]
    v = np.random.standard_normal((G, K, F)) / np.sqrt(K) / s[:, :, None] * t[:, None, :]
    u = np.random.standard_normal((G, F, N)) / np.sqrt(F) / t[:, :, None]
    v_words, v_scales = pack4(v.reshape(G * K, F))
    u_words, u_scales = pack4(u.reshape(G * F, N))
    return {"re": bf(re),
            "im": bf(im),
            "phase": bf(np.random.uniform(0.1, 1.5, (G, F))),
            "v_words": v_words, "v_scales": v_scales,
            "u_words": u_words, "u_scales": u_scales}


def reference(re, im, phase, v_words, v_scales, u_words, u_scales):
    v = unpack4(v_words, v_scales).reshape(G, K, F)
    u = unpack4(u_words, u_scales).reshape(G, F, N)
    a = mxq(f64(re), 2, "e4m3") @ v
    b = mxq(f64(im), 2, "e4m3") @ v
    theta = f64(phase)[:, None, :]
    z = a * np.cos(theta) + b * np.sin(theta)
    return mxq(z, 2, "e4m3") @ u

@@ -1,0 +1,336 @@
+from contextlib import ExitStack
+import math
+
+import concourse.mybir as mybir
+from concourse.masks import make_identity
+
+G, M, K, F, N = 4, 512, 1024, 512, 1024
+FLOPS = 2 * G * (2 * M * K * F + M * F * N)
+
+F32 = mybir.dt.float32
+BF16 = mybir.dt.bfloat16
+U32 = mybir.dt.uint32
+I32 = mybir.dt.int32
+U8 = mybir.dt.uint8
+FP8X4 = mybir.dt.float8_e4m3fn_x4
+FP4X4 = mybir.dt.float4_e2m1fn_x4
+ALU = mybir.AluOpType
+ACT = mybir.ActivationFunctionType
+P = 128
+
+
+def tile_split_real_schrodinger_step_s14_kernel(tc, re, im, phase, v_words, v_scales, u_words, u_scales, out):
+    nc = tc.nc
+    with ExitStack() as ctx:
+        keep = ctx.enter_context(tc.tile_pool(name="keep", bufs=1))
+        work = ctx.enter_context(tc.tile_pool(name="work", bufs=3))
+        psum = ctx.enter_context(tc.psum_pool(name="psum", bufs=8))
+        ctx.enter_context(tc.manual_schedule())
+
+        x = {}
+        for c in range(G):
+            for part in range(2):
+                xt = keep.tile([P, 4, K], BF16, name="x%d_%d" % (c, part))
+                x[c, part] = xt
+        vraw = []
+        vperm = []
+        u = []
+        for c in range(G):
+            t0 = keep.tile([P, 2, 1024], U8, name="vraw%d" % c, align_bytes=64)
+            t1 = keep.tile([P, 2, 4, 256], U8, name="vperm%d" % c, align_bytes=64)
+            t2 = keep.tile([P, 2048], U8, name="u%d" % c, align_bytes=64)
+            vraw.append(t0)
+            vperm.append(t1)
+            u.append(t2)
+        sraw = keep.tile([P, 8, 512], U8, name="sraw", align_bytes=64)
+        sperm = []
+        for c in range(G):
+            t3 = keep.tile([P, 2, 4, 128], U8, name="sperm%d" % c, align_bytes=64)
+            sperm.append(t3)
+        us = keep.tile([P, 4, 1024], U8, name="us", align_bytes=64)
+        ident = keep.tile([P, P], F32, name="ident")
+        ph = keep.tile([P, G, 4], BF16, name="ph")
+        turns = keep.tile([P, G * 4], I32, name="turns")
+        arg = keep.tile([P, 2, G * 4], F32, name="arg")
+        mag = keep.tile([P, G * 4], F32, name="mag")
+        low = keep.tile([P, G * 4], F32, name="low")
+        sc = keep.tile([P, 2, G * 4], F32, name="sc")
+        dummy = keep.tile([P, 1], F32, name="dummy")
+
+        src = (re, im)
+
+        def load_rows(c, part, i0, i1):
+            nc.sync.dma_start(out=x[c, part][:, i0:i1, :], in_=src[part][c].rearrange("(p i) k -> p i k", i=4)[:, i0:i1, :])
+
+        def load_all(c, part):
+            load_rows(c, part, 0, 4)
+
+        def load_v(c):
+            nc.sync.dma_start(out=vraw[c][:].bitcast(I32), in_=v_words[2 * c : 2 * c + 2].bitcast(I32).rearrange("g p b -> p g b"))
+
+        def load_u(c):
+            nc.sync.dma_start(out=u[c][:].bitcast(I32), in_=u_words[c].bitcast(I32))
+
+        nc.vector.memset(sraw[:].bitcast(I32), 0)
+        nc.vector.memset(dummy[:], 0.0)
+        nc.scalar.activation(out=dummy[:], in_=dummy[:], func=ACT.Sin)
+        nc.gpsimd.dma_start(out=ph[:], in_=phase.rearrange("c (p t) -> p c t", t=4))
+        make_identity(nc, ident[:])
+        nc.gpsimd.memset(us[:].bitcast(I32), 0)
+
+        load_rows(0, 0, 0, 1)
+        load_rows(0, 0, 1, 2)
+        load_v(0)
+        load_rows(0, 0, 2, 4)
+        for q in range(4):
+            nc.scalar.dma_start(
+                out=sraw[:].bitcast(I32)[32 * q : 32 * q + 4, :, :],
+                in_=v_scales.bitcast(I32)[:, 4 * q : 4 * q + 4, :].rearrange("g r n -> r g n"),
+            )
+        load_rows(0, 1, 0, 2)
+        load_rows(0, 1, 2, 4)
+        load_all(1, 0)
+        load_v(1)
+        load_all(1, 1)
+        load_u(0)
+        for q in range(4):
+            nc.sync.dma_start(
+                out=us[:].bitcast(I32)[32 * q : 32 * q + 4, :, :],
+                in_=u_scales.bitcast(I32)[:, 4 * q : 4 * q + 4, :].rearrange("c r n -> r c n"),
+            )
+        load_all(2, 0)
+        load_v(2)
+        load_all(2, 1)
+        load_u(1)
+        load_all(3, 0)
+        load_v(3)
+        load_all(3, 1)
+        load_u(2)
+        load_u(3)
+
+        def trig():
+            phf = ph[:].rearrange("p c t -> p (c t)")
+            nc.vector.tensor_scalar(out=turns[:], in0=phf, scalar1=1.0 / (2.0 * math.pi), scalar2=None, op0=ALU.mult)
+            nc.vector.scalar_tensor_tensor(out=arg[:, 0, :], in0=turns[:], scalar=-2.0 * math.pi, in1=phf, op0=ALU.mult, op1=ALU.add)
+            nc.vector.tensor_scalar(out=mag[:], in0=arg[:, 0, :], scalar1=math.pi, scalar2=-2.0 * math.pi, op0=ALU.is_gt, op1=ALU.mult)
+            nc.vector.tensor_scalar(out=low[:], in0=arg[:, 0, :], scalar1=-math.pi, scalar2=2.0 * math.pi, op0=ALU.is_lt, op1=ALU.mult)
+            nc.vector.tensor_tensor(out=arg[:, 0, :], in0=arg[:, 0, :], in1=mag[:], op=ALU.add)
+            nc.vector.tensor_tensor(out=arg[:, 0, :], in0=arg[:, 0, :], in1=low[:], op=ALU.add)
+            nc.vector.scalar_tensor_tensor(out=mag[:], in0=arg[:, 0, :], scalar=-1.0, in1=arg[:, 0, :], op0=ALU.mult, op1=ALU.max)
+            nc.vector.tensor_scalar(out=arg[:, 1, :], in0=mag[:], scalar1=-1.0, scalar2=0.5 * math.pi, op0=ALU.mult, op1=ALU.add)
+            nc.scalar.activation(out=sc[:], in_=arg[:], func=ACT.Sin)
+
+        def bank():
+            b = psum.tile([P, 512], F32, name="bank")
+            return b
+
+        grouped = {}
+        codes = {}
+        scales = {}
+
+        def new_unit(c, part):
+            gt = work.tile([P, 2, 2048], BF16, name="grouped", align_bytes=64)
+            ct = work.tile([P, 2, 512], U32, name="codes", align_bytes=64)
+            st = work.tile([P, 2, 512], U8, name="scales", align_bytes=64)
+            grouped[c, part] = gt
+            codes[c, part] = ct
+            scales[c, part] = st
+
+        def turn(c, part, i, on_vector=False):
+            words = x[c, part][:].bitcast(F32)
+            b = bank()
+            bv = b[:].rearrange("p (g u r) -> p g u r", g=2, u=2)
+            for g in range(2):
+                for e in range(2):
+                    nc.tensor.transpose(bv[:, g, e, :], words[:, i, 256 * g + e : 256 * (g + 1) : 2], ident[:])
+            dst = grouped[c, part][:].bitcast(F32).rearrange("p g (n u) -> p g n u", u=2)[:, :, 128 * i : 128 * (i + 1), :]
+            s = b[:].rearrange("p (g u r) -> p g r u", g=2, u=2)
+            if on_vector:
+                nc.vector.tensor_copy(out=dst, in_=s)
+            else:
+                nc.scalar.copy(out=dst, in_=s)
+
+        def quantize(c, part, g, i0=0, i1=4):
+            cols = slice(128 * i0, 128 * i1)
+            nc.vector.quantize_mx(
+                out=codes[c, part][:, g, cols].bitcast(FP8X4), scales=scales[c, part][:, g, cols],
+                in_=grouped[c, part][:, g, 512 * i0 : 512 * i1],
+            )
+
+        def permute(c):
+            for g in range(2):
+                nc.vector.tensor_copy(
+                    out=vperm[c][:, g, :, :].rearrange("p t (m b) -> p t m b", b=2),
+                    in_=vraw[c][:, g, :].rearrange("p (m t b) -> p t m b", t=4, b=2),
+                )
+            nc.vector.tensor_copy(out=sperm[c][:], in_=sraw[:, 2 * c : 2 * c + 2, :].rearrange("p g (m t) -> p g t m", t=4))
+
+        def project(c, part, t):
+            b = bank()
+            for g in range(2):
+                nc.tensor.matmul_mx(
+                    out=b[:],
+                    lhsT=vperm[c][:, g, t, :].bitcast(FP4X4),
+                    lhsT_scale=sperm[c][:, g, t, :],
+                    rhs=codes[c, part][:, g, :].bitcast(FP8X4),
+                    rhs_scale=scales[c, part][:, g, :],
+                    start=(g == 0),
+                    stop=(g == 1),
+                )
+            return b
+
+        acos = {}
+        zrows = {}
+        zgroup = {}
+        zcodes = {}
+        zscales = {}
+
+        def real_part(c, t):
+            b = project(c, 0, t)
+            a = work.tile([P, 512], F32, name="acos", bufs=5)
+            acos[c, t] = a
+            nc.scalar.activation(out=a[:], in_=b[:], func=ACT.Copy, scale=sc[:, 1, 4 * c + t : 4 * c + t + 1])
+
+        def new_z(c):
+            z0 = work.tile([P, 4, 512], BF16, name="zrows", bufs=2)
+            z1 = work.tile([P, 512, 4], BF16, name="zgroup", bufs=2, align_bytes=64)
+            z2 = work.tile([P, 512], U32, name="zcodes", bufs=2, align_bytes=64)
+            z3 = work.tile([P, 512], U8, name="zscales", bufs=2, align_bytes=64)
+            zrows[c] = z0
+            zgroup[c] = z1
+            zcodes[c] = z2
+            zscales[c] = z3
+
+        def add_imag(c, t, cols, b):
+            nc.vector.scalar_tensor_tensor(
+                out=zrows[c][:, t, cols], in0=b, scalar=sc[:, 0, 4 * c + t : 4 * c + t + 1], in1=acos[c, t][:, cols],
+                op0=ALU.mult, op1=ALU.add,
+            )
+
+        def imag_part(c, t):
+            b = project(c, 1, t)
+            add_imag(c, t, slice(0, 512), b[:])
+
+        def imag_rows(c, i):
+            cols = slice(128 * i, 128 * (i + 1))
+            b = bank()
+            for t in range(4):
+                for g in range(2):
+                    nc.tensor.matmul_mx(
+                        out=b[:, 128 * t : 128 * (t + 1)],
+                        lhsT=vperm[c][:, g, t, :].bitcast(FP4X4),
+                        lhsT_scale=sperm[c][:, g, t, :],
+                        rhs=codes[c, 1][:, g, cols].bitcast(FP8X4),
+                        rhs_scale=scales[c, 1][:, g, cols],
+                        start=(g == 0),
+                        stop=(g == 1),
+                    )
+            return b
+
+        def add_imag_rows(c, i, b):
+            for t in range(4):
+                add_imag(c, t, slice(128 * i, 128 * (i + 1)), b[:, 128 * t : 128 * (t + 1)])
+
+        def interleave(c, i):
+            cols = slice(128 * i, 128 * (i + 1))
+            nc.vector.tensor_copy(out=zgroup[c][:, cols, :], in_=zrows[c][:, :, cols].rearrange("p t n -> p n t"))
+
+        def quantize_z(c, i):
+            cols = slice(128 * i, 128 * (i + 1))
+            nc.vector.quantize_mx(
+                out=zcodes[c][:, cols].bitcast(FP8X4), scales=zscales[c][:, cols],
+                in_=zgroup[c][:, cols, :].rearrange("p n t -> p (n t)"),
+            )
+
+        out_rows = {}
+
+        def expand(c, i, n, on_vector):
+            cols = slice(128 * i, 128 * (i + 1))
+            b = bank()
+            nc.tensor.matmul_mx(
+                out=b[:],
+                lhsT=zcodes[c][:, cols].bitcast(FP8X4),
+                lhsT_scale=zscales[c][:, cols],
+                rhs=u[c][:, 1024 * n : 1024 * (n + 1)].bitcast(FP4X4),
+                rhs_scale=us[:, c, 512 * n : 512 * (n + 1)],
+                start=True,
+                stop=True,
+            )
+            if n == 0:
+                o = work.tile([P, 1024], F32, name="orow", bufs=6)
+                out_rows[c, i] = o
+            dst = out_rows[c, i][:, 512 * n : 512 * (n + 1)]
+            if on_vector:
+                nc.vector.tensor_copy(out=dst, in_=b[:])
+            else:
+                nc.scalar.copy(out=dst, in_=b[:])
+            if n == 1:
+                nc.sync.dma_start(out=out[c].rearrange("(p i) n -> p i n", i=4)[:, i, :], in_=out_rows[c, i][:])
+
+        new_unit(0, 0)
+        new_unit(0, 1)
+        trig()
+        for i in range(4):
+            turn(0, 0, i)
+        permute(0)
+        for i in range(0, 4, 2):
+            for g in range(2):
+                quantize(0, 0, g, i, i + 2)
+        for i in range(3):
+            turn(0, 1, i, on_vector=(i == 1))
+        for t in range(4):
+            real_part(0, t)
+        turn(0, 1, 3, on_vector=True)
+        for c in range(G - 1):
+            new_unit(c + 1, 0)
+            for i in range(4):
+                turn(c + 1, 0, i)
+            if c == 0:
+                quantize(0, 1, 0)
+                quantize(0, 1, 1)
+            permute(c + 1)
+            new_z(c)
+            for t in range(4):
+                imag_part(c, t)
+            quantize(c + 1, 0, 0)
+            interleave(c, 0)
+            interleave(c, 1)
+            quantize_z(c, 0)
+            interleave(c, 2)
+            quantize_z(c, 1)
+            interleave(c, 3)
+            quantize_z(c, 2)
+            quantize_z(c, 3)
+            new_unit(c + 1, 1)
+            for i in range(4):
+                turn(c + 1, 1, i)
+            quantize(c + 1, 0, 1)
+            for i in range(4 if c + 2 < G else 2):
+                for n in range(2):
+                    expand(c, i, n, on_vector=(n == 1 and i % 2 == 1))
+            quantize(c + 1, 1, 0)
+            quantize(c + 1, 1, 1)
+            for t in range(4):
+                real_part(c + 1, t)
+
+        c = G - 1
+        new_z(c)
+        b = {}
+        b = imag_rows(c, 0)
+        add_imag_rows(c, 0, b)
+        expand(c - 1, 2, 0, on_vector=True)
+        expand(c - 1, 2, 1, on_vector=False)
+        for i in range(1, 4):
+            b = imag_rows(c, i)
+            interleave(c, i - 1)
+            add_imag_rows(c, i, b)
+            quantize_z(c, i - 1)
+            j, d = (c - 1, 3) if i == 1 else (c, i - 2)
+            expand(j, d, 0, on_vector=False)
+            expand(j, d, 1, on_vector=False)
+        interleave(c, 3)
+        quantize_z(c, 3)
+        expand(c, 2, 0, on_vector=False)
+        expand(c, 2, 1, on_vector=True)
+        expand(c, 3, 0, on_vector=False)
+        expand(c, 3, 1, on_vector=True)

@@ -18,6 +18,28 @@ ALU = mybir.AluOpType
 ACT = mybir.ActivationFunctionType
 P = 128
 
+PLAN = (
+    "T000 T001 T002 T003 T010 T011 ET000S pc00 pc01 ET002S T012 ps0 ET001V Q0010 "
+    "Q0000 ET003S Q0001 Q0011 ps3 T013 ET013S ET011S ps1 T100 ET100S ET010S T101 ET101S "
+    "A02 EA02 T102 ET102S ET012V Q010 T110 ET110S T103 ET103S T111 ET111S A01 EA01 "
+    "Q011 B02 A00 EA00 pc10 A03 EA03 ps2 EB02 pc11 B00 EB00 pc20 B01 "
+    "EB01 T202 ET202S T113 ET113S T112 ET112S T201 ET201S Q100 B03 T210 ET210S T212 "
+    "ET212S T301 ET301S Q101 A10 A11 A12 A13 EA10 EA11 EA12 EA13 EB03 IL00 "
+    "IL01 IL02 IL03 QZ00 QZ01 QZ02 QZ03 O001 EO001S pc21 T302 ET302S Q110 T203 "
+    "ET203S T313 ET313S O031 EO031S Q111 B10 B11 B12 B13 EB10 EB11 EB12 EB13 "
+    "IL10 IL11 IL12 IL13 QZ10 QZ11 QZ12 QZ13 T213 ET213S T200 ET200S Q200 Q201 "
+    "T310 ET310S T312 ET312S O010 EO010S T211 ET211S Q210 Q211 T300 ET300S T303 ET303S "
+    "Q300 Q301 pc30 O000 EO000S O020 EO020S O101 EO101S A22 EA22 A20 EA20 O011 "
+    "EO011V B22 EB22 B20 EB20 O121 EO121S A23 EA23 pc31 O131 EO131V O030 EO030S "
+    "T311 ET311S Q310 Q311 O021 EO021S O130 EO130S A21 EA21 B23 EB23 O111 EO111S "
+    "O100 EO100S B21 EB21 IL20 IL21 IL23 QZ20 A33 EA33 IL22 O120 EO120S A32 "
+    "EA32 O110 EO110V A30 EA30 A31 EA31 B31 O201 EO201S O200 EO200S B30 QZ21 "
+    "O210 O211 EO210S EO211S EB31 B33 QZ23 O230 O231 EO230S EO231S EB30 IL30 IL31 "
+    "QZ30 QZ31 O300 O301 O310 O311 EO300V EO301S EO310S EO311S EB33 B32 QZ22 O220 "
+    "O221 EO220S EO221S EB32 IL32 IL33 QZ32 QZ33 O320 O321 O330 O331 EO320S EO321V "
+    "EO330S EO331V "
+)
+
 
 def tile_split_real_schrodinger_step_s14_kernel(tc, re, im, phase, v_words, v_scales, u_words, u_scales, out):
     nc = tc.nc
@@ -74,19 +96,19 @@ def tile_split_real_schrodinger_step_s14_kernel(tc, re, im, phase, v_words, v_sc
         nc.vector.memset(sraw[:].bitcast(I32), 0)
         nc.vector.memset(dummy[:], 0.0)
         nc.scalar.activation(out=dummy[:], in_=dummy[:], func=ACT.Sin)
-        nc.gpsimd.dma_start(out=ph[:], in_=phase.rearrange("c (p t) -> p c t", t=4))
         make_identity(nc, ident[:])
         nc.gpsimd.memset(us[:].bitcast(I32), 0)
 
-        load_rows(0, 0, 0, 1)
-        load_rows(0, 0, 1, 2)
         load_v(0)
-        load_rows(0, 0, 2, 4)
+        load_rows(0, 0, 0, 1)
+        load_rows(0, 0, 1, 3)
+        nc.scalar.dma_start(out=ph[:], in_=phase.rearrange("c (p t) -> p c t", t=4))
         for q in range(4):
             nc.scalar.dma_start(
                 out=sraw[:].bitcast(I32)[32 * q : 32 * q + 4, :, :],
                 in_=v_scales.bitcast(I32)[:, 4 * q : 4 * q + 4, :].rearrange("g r n -> r g n"),
             )
+        load_rows(0, 0, 3, 4)
         load_rows(0, 1, 0, 2)
         load_rows(0, 1, 2, 4)
         load_all(1, 0)
@@ -108,16 +130,32 @@ def tile_split_real_schrodinger_step_s14_kernel(tc, re, im, phase, v_words, v_sc
         load_u(2)
         load_u(3)
 
-        def trig():
-            phf = ph[:].rearrange("p c t -> p (c t)")
+        phf = ph[:].rearrange("p c t -> p (c t)")
+        angle = arg[:, 0, :]
+
+        def trig_turns():
             nc.vector.tensor_scalar(out=turns[:], in0=phf, scalar1=1.0 / (2.0 * math.pi), scalar2=None, op0=ALU.mult)
-            nc.vector.scalar_tensor_tensor(out=arg[:, 0, :], in0=turns[:], scalar=-2.0 * math.pi, in1=phf, op0=ALU.mult, op1=ALU.add)
-            nc.vector.tensor_scalar(out=mag[:], in0=arg[:, 0, :], scalar1=math.pi, scalar2=-2.0 * math.pi, op0=ALU.is_gt, op1=ALU.mult)
-            nc.vector.tensor_scalar(out=low[:], in0=arg[:, 0, :], scalar1=-math.pi, scalar2=2.0 * math.pi, op0=ALU.is_lt, op1=ALU.mult)
-            nc.vector.tensor_tensor(out=arg[:, 0, :], in0=arg[:, 0, :], in1=mag[:], op=ALU.add)
-            nc.vector.tensor_tensor(out=arg[:, 0, :], in0=arg[:, 0, :], in1=low[:], op=ALU.add)
-            nc.vector.scalar_tensor_tensor(out=mag[:], in0=arg[:, 0, :], scalar=-1.0, in1=arg[:, 0, :], op0=ALU.mult, op1=ALU.max)
+
+        def trig_reduce():
+            nc.vector.scalar_tensor_tensor(out=angle, in0=turns[:], scalar=-2.0 * math.pi, in1=phf, op0=ALU.mult, op1=ALU.add)
+
+        def trig_wraps():
+            nc.vector.tensor_scalar(out=mag[:], in0=angle, scalar1=math.pi, scalar2=-2.0 * math.pi, op0=ALU.is_gt, op1=ALU.mult)
+            nc.vector.tensor_scalar(out=low[:], in0=angle, scalar1=-math.pi, scalar2=2.0 * math.pi, op0=ALU.is_lt, op1=ALU.mult)
+
+        def trig_wrap_high():
+            nc.vector.tensor_tensor(out=angle, in0=angle, in1=mag[:], op=ALU.add)
+
+        def trig_wrap_low():
+            nc.vector.tensor_tensor(out=angle, in0=angle, in1=low[:], op=ALU.add)
+
+        def trig_magnitude():
+            nc.vector.scalar_tensor_tensor(out=mag[:], in0=angle, scalar=-1.0, in1=angle, op0=ALU.mult, op1=ALU.max)
+
+        def trig_cos_angle():
             nc.vector.tensor_scalar(out=arg[:, 1, :], in0=mag[:], scalar1=-1.0, scalar2=0.5 * math.pi, op0=ALU.mult, op1=ALU.add)
+
+        def trig_sin():
             nc.scalar.activation(out=sc[:], in_=arg[:], func=ACT.Sin)
 
         def bank():
@@ -129,26 +167,50 @@ def tile_split_real_schrodinger_step_s14_kernel(tc, re, im, phase, v_words, v_sc
         scales = {}
 
         def new_unit(c, part):
-            gt = work.tile([P, 2, 2048], BF16, name="grouped", align_bytes=64)
-            ct = work.tile([P, 2, 512], U32, name="codes", align_bytes=64)
-            st = work.tile([P, 2, 512], U8, name="scales", align_bytes=64)
+            gt = work.tile([P, 2, 2048], BF16, name="grouped", bufs=5, align_bytes=64)
+            ct = work.tile([P, 2, 512], U32, name="codes", bufs=5, align_bytes=64)
+            st = work.tile([P, 2, 512], U8, name="scales", bufs=5, align_bytes=64)
             grouped[c, part] = gt
             codes[c, part] = ct
             scales[c, part] = st
 
-        def turn(c, part, i, on_vector=False):
+        sorted_words = {}
+
+        def sort_words(c, part, i):
+            w = work.tile([P, 512], F32, name="sorted_words", bufs=3)
+            sorted_words[c, part, i] = w
+            nc.vector.tensor_copy(
+                out=w[:].rearrange("p (g u r) -> p g u r", g=2, u=2),
+                in_=x[c, part][:].bitcast(F32)[:, i, :].rearrange("p (g r u) -> p g u r", g=2, u=2),
+            )
+
+        banks = {}
+
+        def turn(c, part, i):
             words = x[c, part][:].bitcast(F32)
             b = bank()
+            banks["T", c, part, i] = b
             bv = b[:].rearrange("p (g u r) -> p g u r", g=2, u=2)
             for g in range(2):
                 for e in range(2):
-                    nc.tensor.transpose(bv[:, g, e, :], words[:, i, 256 * g + e : 256 * (g + 1) : 2], ident[:])
-            dst = grouped[c, part][:].bitcast(F32).rearrange("p g (n u) -> p g n u", u=2)[:, :, 128 * i : 128 * (i + 1), :]
-            s = b[:].rearrange("p (g u r) -> p g r u", g=2, u=2)
+                    if (c, part, i) in sorted_words:
+                        w0 = 256 * g + 128 * e
+                        source = sorted_words[c, part, i][:, w0 : w0 + 128]
+                    else:
+                        source = words[:, i, 256 * g + e : 256 * (g + 1) : 2]
+                    nc.tensor.transpose(bv[:, g, e, :], source, ident[:])
+
+        def copy_out(dst, s, on_vector):
             if on_vector:
                 nc.vector.tensor_copy(out=dst, in_=s)
             else:
                 nc.scalar.copy(out=dst, in_=s)
+
+        def turn_out(c, part, i, on_vector):
+            if (c, part) not in grouped:
+                new_unit(c, part)
+            dst = grouped[c, part][:].bitcast(F32).rearrange("p g (n u) -> p g n u", u=2)[:, :, 128 * i : 128 * (i + 1), :]
+            copy_out(dst, banks["T", c, part, i][:].rearrange("p (g u r) -> p g r u", g=2, u=2), on_vector)
 
         def quantize(c, part, g, i0=0, i1=4):
             cols = slice(128 * i0, 128 * i1)
@@ -157,12 +219,18 @@ def tile_split_real_schrodinger_step_s14_kernel(tc, re, im, phase, v_words, v_sc
                 in_=grouped[c, part][:, g, 512 * i0 : 512 * i1],
             )
 
-        def permute(c):
+        def permute_codes(c):
             for g in range(2):
+                permute_group(c, g)
+
+        def permute_group(c, g):
+            if True:
                 nc.vector.tensor_copy(
                     out=vperm[c][:, g, :, :].rearrange("p t (m b) -> p t m b", b=2),
                     in_=vraw[c][:, g, :].rearrange("p (m t b) -> p t m b", t=4, b=2),
                 )
+
+        def permute_scales(c):
             nc.vector.tensor_copy(out=sperm[c][:], in_=sraw[:, 2 * c : 2 * c + 2, :].rearrange("p g (m t) -> p g t m", t=4))
 
         def project(c, part, t):
@@ -185,11 +253,10 @@ def tile_split_real_schrodinger_step_s14_kernel(tc, re, im, phase, v_words, v_sc
         zcodes = {}
         zscales = {}
 
-        def real_part(c, t):
-            b = project(c, 0, t)
-            a = work.tile([P, 512], F32, name="acos", bufs=5)
+        def real_out(c, t):
+            a = work.tile([P, 512], F32, name="acos", bufs=6)
             acos[c, t] = a
-            nc.scalar.activation(out=a[:], in_=b[:], func=ACT.Copy, scale=sc[:, 1, 4 * c + t : 4 * c + t + 1])
+            nc.scalar.activation(out=a[:], in_=banks["A", c, t][:], func=ACT.Copy, scale=sc[:, 1, 4 * c + t : 4 * c + t + 1])
 
         def new_z(c):
             z0 = work.tile([P, 4, 512], BF16, name="zrows", bufs=2)
@@ -202,34 +269,35 @@ def tile_split_real_schrodinger_step_s14_kernel(tc, re, im, phase, v_words, v_sc
             zscales[c] = z3
 
         def add_imag(c, t, cols, b):
+            if c not in zrows:
+                new_z(c)
             nc.vector.scalar_tensor_tensor(
                 out=zrows[c][:, t, cols], in0=b, scalar=sc[:, 0, 4 * c + t : 4 * c + t + 1], in1=acos[c, t][:, cols],
                 op0=ALU.mult, op1=ALU.add,
             )
 
-        def imag_part(c, t):
-            b = project(c, 1, t)
-            add_imag(c, t, slice(0, 512), b[:])
-
-        def imag_rows(c, i):
-            cols = slice(128 * i, 128 * (i + 1))
+        def imag_half(c, h, j):
             b = bank()
-            for t in range(4):
-                for g in range(2):
-                    nc.tensor.matmul_mx(
-                        out=b[:, 128 * t : 128 * (t + 1)],
-                        lhsT=vperm[c][:, g, t, :].bitcast(FP4X4),
-                        lhsT_scale=sperm[c][:, g, t, :],
-                        rhs=codes[c, 1][:, g, cols].bitcast(FP8X4),
-                        rhs_scale=scales[c, 1][:, g, cols],
-                        start=(g == 0),
-                        stop=(g == 1),
-                    )
-            return b
+            banks["B", c, 2 * h + j] = b
+            for k in range(2):
+                t = 2 * j + k
+                for r in range(2):
+                    cols = slice(256 * h + 128 * r, 256 * h + 128 * (r + 1))
+                    for g in range(2):
+                        nc.tensor.matmul_mx(
+                            out=b[:, 256 * k + 128 * r : 256 * k + 128 * (r + 1)],
+                            lhsT=vperm[c][:, g, t, :].bitcast(FP4X4),
+                            lhsT_scale=sperm[c][:, g, t, :],
+                            rhs=codes[c, 1][:, g, cols].bitcast(FP8X4),
+                            rhs_scale=scales[c, 1][:, g, cols],
+                            start=(g == 0),
+                            stop=(g == 1),
+                        )
 
-        def add_imag_rows(c, i, b):
-            for t in range(4):
-                add_imag(c, t, slice(128 * i, 128 * (i + 1)), b[:, 128 * t : 128 * (t + 1)])
+        def add_imag_half(c, h, j):
+            b = banks["B", c, 2 * h + j]
+            for k in range(2):
+                add_imag(c, 2 * j + k, slice(256 * h, 256 * (h + 1)), b[:, 256 * k : 256 * (k + 1)])
 
         def interleave(c, i):
             cols = slice(128 * i, 128 * (i + 1))
@@ -244,9 +312,10 @@ def tile_split_real_schrodinger_step_s14_kernel(tc, re, im, phase, v_words, v_sc
 
         out_rows = {}
 
-        def expand(c, i, n, on_vector):
+        def expand(c, i, n):
             cols = slice(128 * i, 128 * (i + 1))
             b = bank()
+            banks["O", c, i, n] = b
             nc.tensor.matmul_mx(
                 out=b[:],
                 lhsT=zcodes[c][:, cols].bitcast(FP8X4),
@@ -256,81 +325,52 @@ def tile_split_real_schrodinger_step_s14_kernel(tc, re, im, phase, v_words, v_sc
                 start=True,
                 stop=True,
             )
-            if n == 0:
-                o = work.tile([P, 1024], F32, name="orow", bufs=6)
+
+        def expand_out(c, i, n, on_vector):
+            second = (c, i) in out_rows
+            if not second:
+                o = work.tile([P, 1024], F32, name="orow", bufs=8)
                 out_rows[c, i] = o
-            dst = out_rows[c, i][:, 512 * n : 512 * (n + 1)]
-            if on_vector:
-                nc.vector.tensor_copy(out=dst, in_=b[:])
-            else:
-                nc.scalar.copy(out=dst, in_=b[:])
-            if n == 1:
+            copy_out(out_rows[c, i][:, 512 * n : 512 * (n + 1)], banks["O", c, i, n][:], on_vector)
+            if second:
                 nc.sync.dma_start(out=out[c].rearrange("(p i) n -> p i n", i=4)[:, i, :], in_=out_rows[c, i][:])
 
-        new_unit(0, 0)
-        new_unit(0, 1)
-        trig()
-        for i in range(4):
-            turn(0, 0, i)
-        permute(0)
-        for i in range(0, 4, 2):
-            for g in range(2):
-                quantize(0, 0, g, i, i + 2)
-        for i in range(3):
-            turn(0, 1, i, on_vector=(i == 1))
-        for t in range(4):
-            real_part(0, t)
-        turn(0, 1, 3, on_vector=True)
-        for c in range(G - 1):
-            new_unit(c + 1, 0)
-            for i in range(4):
-                turn(c + 1, 0, i)
-            if c == 0:
-                quantize(0, 1, 0)
-                quantize(0, 1, 1)
-            permute(c + 1)
-            new_z(c)
-            for t in range(4):
-                imag_part(c, t)
-            quantize(c + 1, 0, 0)
-            interleave(c, 0)
-            interleave(c, 1)
-            quantize_z(c, 0)
-            interleave(c, 2)
-            quantize_z(c, 1)
-            interleave(c, 3)
-            quantize_z(c, 2)
-            quantize_z(c, 3)
-            new_unit(c + 1, 1)
-            for i in range(4):
-                turn(c + 1, 1, i)
-            quantize(c + 1, 0, 1)
-            for i in range(4 if c + 2 < G else 2):
-                for n in range(2):
-                    expand(c, i, n, on_vector=(n == 1 and i % 2 == 1))
-            quantize(c + 1, 1, 0)
-            quantize(c + 1, 1, 1)
-            for t in range(4):
-                real_part(c + 1, t)
-
-        c = G - 1
-        new_z(c)
-        b = {}
-        b = imag_rows(c, 0)
-        add_imag_rows(c, 0, b)
-        expand(c - 1, 2, 0, on_vector=True)
-        expand(c - 1, 2, 1, on_vector=False)
-        for i in range(1, 4):
-            b = imag_rows(c, i)
-            interleave(c, i - 1)
-            add_imag_rows(c, i, b)
-            quantize_z(c, i - 1)
-            j, d = (c - 1, 3) if i == 1 else (c, i - 2)
-            expand(j, d, 0, on_vector=False)
-            expand(j, d, 1, on_vector=False)
-        interleave(c, 3)
-        quantize_z(c, 3)
-        expand(c, 2, 0, on_vector=False)
-        expand(c, 2, 1, on_vector=True)
-        expand(c, 3, 0, on_vector=False)
-        expand(c, 3, 1, on_vector=True)
+        trig = [trig_turns, trig_reduce, trig_wraps, trig_wrap_high, trig_wrap_low, trig_magnitude, trig_cos_angle]
+        steps = {"pc": permute_group, "ps": permute_scales, "sort": sort_words, "T": turn, "ET": turn_out, "EA": real_out, "IL": interleave, "QZ": quantize_z, "O": expand, "EO": expand_out}
+        vector_steps = 0
+        sine_done = False
+        for token in PLAN.split():
+            name = "".join([ch for ch in token if ch not in "0123456789" and not (ch in "SV" and len(token) > 4)])
+            args = [int(ch) for ch in token if ch in "0123456789"]
+            if name == "ET" or name == "EO":
+                args.append(token[len(token) - 1 :] == "V")
+            if name == "EA" and not sine_done:
+                for f in trig:
+                    f()
+                trig = []
+                trig_sin()
+                sine_done = True
+            if name in steps:
+                steps[name](*args)
+            elif name == "Q":
+                if len(args) == 4:
+                    quantize(args[0], args[1], args[2], 2 * args[3], 2 * args[3] + 2)
+                else:
+                    quantize(*args)
+            elif name == "A":
+                banks["A", args[0], args[1]] = project(args[0], 0, args[1])
+            elif name == "B":
+                if args[0] < G - 1:
+                    banks["B", args[0], args[1]] = project(args[0], 1, args[1])
+                else:
+                    imag_half(args[0], args[1] // 2, args[1] % 2)
+            elif name == "EB":
+                if args[0] < G - 1:
+                    add_imag(args[0], args[1], slice(0, 512), banks["B", args[0], args[1]][:])
+                else:
+                    add_imag_half(args[0], args[1] // 2, args[1] % 2)
+            if name in ("pc", "ps", "sort", "Q", "IL", "QZ", "EB") or token[len(token) - 1 :] == "V":
+                vector_steps += 1
+                if vector_steps > 2 and trig:
+                    trig[0]()
+                    trig = trig[1:]

@@ -18,28 +18,6 @@ ALU = mybir.AluOpType
 ACT = mybir.ActivationFunctionType
 P = 128
 
-PLAN = (
-    "T000 T001 T002 T003 T010 T011 ET000S pc00 pc01 ET002S T012 ps0 ET001V Q0010 "
-    "Q0000 ET003S Q0001 Q0011 ps3 T013 ET013S ET011S ps1 T100 ET100S ET010S T101 ET101S "
-    "A02 EA02 T102 ET102S ET012V Q010 T110 ET110S T103 ET103S T111 ET111S A01 EA01 "
-    "Q011 B02 A00 EA00 pc10 A03 EA03 ps2 EB02 pc11 B00 EB00 pc20 B01 "
-    "EB01 T202 ET202S T113 ET113S T112 ET112S T201 ET201S Q100 B03 T210 ET210S T212 "
-    "ET212S T301 ET301S Q101 A10 A11 A12 A13 EA10 EA11 EA12 EA13 EB03 IL00 "
-    "IL01 IL02 IL03 QZ00 QZ01 QZ02 QZ03 O001 EO001S pc21 T302 ET302S Q110 T203 "
-    "ET203S T313 ET313S O031 EO031S Q111 B10 B11 B12 B13 EB10 EB11 EB12 EB13 "
-    "IL10 IL11 IL12 IL13 QZ10 QZ11 QZ12 QZ13 T213 ET213S T200 ET200S Q200 Q201 "
-    "T310 ET310S T312 ET312S O010 EO010S T211 ET211S Q210 Q211 T300 ET300S T303 ET303S "
-    "Q300 Q301 pc30 O000 EO000S O020 EO020S O101 EO101S A22 EA22 A20 EA20 O011 "
-    "EO011V B22 EB22 B20 EB20 O121 EO121S A23 EA23 pc31 O131 EO131V O030 EO030S "
-    "T311 ET311S Q310 Q311 O021 EO021S O130 EO130S A21 EA21 B23 EB23 O111 EO111S "
-    "O100 EO100S B21 EB21 IL20 IL21 IL23 QZ20 A33 EA33 IL22 O120 EO120S A32 "
-    "EA32 O110 EO110V A30 EA30 A31 EA31 B31 O201 EO201S O200 EO200S B30 QZ21 "
-    "O210 O211 EO210S EO211S EB31 B33 QZ23 O230 O231 EO230S EO231S EB30 IL30 IL31 "
-    "QZ30 QZ31 O300 O301 O310 O311 EO300V EO301S EO310S EO311S EB33 B32 QZ22 O220 "
-    "O221 EO220S EO221S EB32 IL32 IL33 QZ32 QZ33 O320 O321 O330 O331 EO320S EO321V "
-    "EO330S EO331V "
-)
-
 
 def tile_split_real_schrodinger_step_s14_kernel(tc, re, im, phase, v_words, v_scales, u_words, u_scales, out):
     nc = tc.nc
@@ -74,8 +52,8 @@ def tile_split_real_schrodinger_step_s14_kernel(tc, re, im, phase, v_words, v_sc
         ph = keep.tile([P, G, 4], BF16, name="ph")
         turns = keep.tile([P, G * 4], I32, name="turns")
         arg = keep.tile([P, 2, G * 4], F32, name="arg")
-        mag = keep.tile([P, G * 4], F32, name="mag")
-        low = keep.tile([P, G * 4], F32, name="low")
+        high = keep.tile([P, 2, G * 4], F32, name="high")
+        low = keep.tile([P, 2, G * 4], F32, name="low")
         sc = keep.tile([P, 2, G * 4], F32, name="sc")
         dummy = keep.tile([P, 1], F32, name="dummy")
 
@@ -99,18 +77,18 @@ def tile_split_real_schrodinger_step_s14_kernel(tc, re, im, phase, v_words, v_sc
         make_identity(nc, ident[:])
         nc.gpsimd.memset(us[:].bitcast(I32), 0)
 
-        load_v(0)
         load_rows(0, 0, 0, 1)
-        load_rows(0, 0, 1, 3)
+        load_rows(0, 0, 1, 2)
+        load_rows(0, 0, 2, 4)
+        load_v(0)
         nc.scalar.dma_start(out=ph[:], in_=phase.rearrange("c (p t) -> p c t", t=4))
+        load_rows(0, 1, 0, 2)
+        load_rows(0, 1, 2, 4)
         for q in range(4):
-            nc.scalar.dma_start(
+            nc.sync.dma_start(
                 out=sraw[:].bitcast(I32)[32 * q : 32 * q + 4, :, :],
                 in_=v_scales.bitcast(I32)[:, 4 * q : 4 * q + 4, :].rearrange("g r n -> r g n"),
             )
-        load_rows(0, 0, 3, 4)
-        load_rows(0, 1, 0, 2)
-        load_rows(0, 1, 2, 4)
         load_all(1, 0)
         load_v(1)
         load_all(1, 1)
@@ -139,21 +117,12 @@ def tile_split_real_schrodinger_step_s14_kernel(tc, re, im, phase, v_words, v_sc
         def trig_reduce():
             nc.vector.scalar_tensor_tensor(out=angle, in0=turns[:], scalar=-2.0 * math.pi, in1=phf, op0=ALU.mult, op1=ALU.add)
 
-        def trig_wraps():
-            nc.vector.tensor_scalar(out=mag[:], in0=angle, scalar1=math.pi, scalar2=-2.0 * math.pi, op0=ALU.is_gt, op1=ALU.mult)
-            nc.vector.tensor_scalar(out=low[:], in0=angle, scalar1=-math.pi, scalar2=2.0 * math.pi, op0=ALU.is_lt, op1=ALU.mult)
-
-        def trig_wrap_high():
-            nc.vector.tensor_tensor(out=angle, in0=angle, in1=mag[:], op=ALU.add)
-
-        def trig_wrap_low():
-            nc.vector.tensor_tensor(out=angle, in0=angle, in1=low[:], op=ALU.add)
-
-        def trig_magnitude():
-            nc.vector.scalar_tensor_tensor(out=mag[:], in0=angle, scalar=-1.0, in1=angle, op0=ALU.mult, op1=ALU.max)
-
-        def trig_cos_angle():
-            nc.vector.tensor_scalar(out=arg[:, 1, :], in0=mag[:], scalar1=-1.0, scalar2=0.5 * math.pi, op0=ALU.mult, op1=ALU.add)
+        def trig_wrap():
+            nc.gpsimd.tensor_scalar(out=arg[:, 1, :], in0=angle, scalar1=1.0, scalar2=0.5 * math.pi, op0=ALU.mult, op1=ALU.add)
+            nc.gpsimd.tensor_scalar(out=high[:], in0=arg[:], scalar1=math.pi, scalar2=-2.0 * math.pi, op0=ALU.is_gt, op1=ALU.mult)
+            nc.gpsimd.tensor_scalar(out=low[:], in0=arg[:], scalar1=-math.pi, scalar2=2.0 * math.pi, op0=ALU.is_lt, op1=ALU.mult)
+            nc.gpsimd.tensor_tensor(out=arg[:], in0=arg[:], in1=high[:], op=ALU.add)
+            nc.gpsimd.tensor_tensor(out=arg[:], in0=arg[:], in1=low[:], op=ALU.add)
 
         def trig_sin():
             nc.scalar.activation(out=sc[:], in_=arg[:], func=ACT.Sin)
@@ -167,9 +136,9 @@ def tile_split_real_schrodinger_step_s14_kernel(tc, re, im, phase, v_words, v_sc
         scales = {}
 
         def new_unit(c, part):
-            gt = work.tile([P, 2, 2048], BF16, name="grouped", bufs=5, align_bytes=64)
-            ct = work.tile([P, 2, 512], U32, name="codes", bufs=5, align_bytes=64)
-            st = work.tile([P, 2, 512], U8, name="scales", bufs=5, align_bytes=64)
+            gt = work.tile([P, 2, 2048], BF16, name="grouped", bufs=4, align_bytes=64)
+            ct = work.tile([P, 2, 512], U32, name="codes", bufs=4, align_bytes=64)
+            st = work.tile([P, 2, 512], U8, name="scales", bufs=4, align_bytes=64)
             grouped[c, part] = gt
             codes[c, part] = ct
             scales[c, part] = st
@@ -331,46 +300,101 @@ def tile_split_real_schrodinger_step_s14_kernel(tc, re, im, phase, v_words, v_sc
             if not second:
                 o = work.tile([P, 1024], F32, name="orow", bufs=8)
                 out_rows[c, i] = o
-            copy_out(out_rows[c, i][:, 512 * n : 512 * (n + 1)], banks["O", c, i, n][:], on_vector)
-            if second:
+            cols = slice(512 * n, 512 * (n + 1))
+            copy_out(out_rows[c, i][:, cols], banks["O", c, i, n][:], on_vector)
+            if c == 3:
+                nc.sync.dma_start(out=out[c].rearrange("(p i) n -> p i n", i=4)[:, i, cols], in_=out_rows[c, i][:, cols])
+            elif second:
                 nc.sync.dma_start(out=out[c].rearrange("(p i) n -> p i n", i=4)[:, i, :], in_=out_rows[c, i][:])
 
-        trig = [trig_turns, trig_reduce, trig_wraps, trig_wrap_high, trig_wrap_low, trig_magnitude, trig_cos_angle]
-        steps = {"pc": permute_group, "ps": permute_scales, "sort": sort_words, "T": turn, "ET": turn_out, "EA": real_out, "IL": interleave, "QZ": quantize_z, "O": expand, "EO": expand_out}
-        vector_steps = 0
-        sine_done = False
-        for token in PLAN.split():
-            name = "".join([ch for ch in token if ch not in "0123456789" and not (ch in "SV" and len(token) > 4)])
-            args = [int(ch) for ch in token if ch in "0123456789"]
-            if name == "ET" or name == "EO":
-                args.append(token[len(token) - 1 :] == "V")
-            if name == "EA" and not sine_done:
-                for f in trig:
-                    f()
-                trig = []
-                trig_sin()
-                sine_done = True
-            if name in steps:
-                steps[name](*args)
-            elif name == "Q":
-                if len(args) == 4:
-                    quantize(args[0], args[1], args[2], 2 * args[3], 2 * args[3] + 2)
-                else:
-                    quantize(*args)
-            elif name == "A":
-                banks["A", args[0], args[1]] = project(args[0], 0, args[1])
-            elif name == "B":
-                if args[0] < G - 1:
-                    banks["B", args[0], args[1]] = project(args[0], 1, args[1])
-                else:
-                    imag_half(args[0], args[1] // 2, args[1] % 2)
-            elif name == "EB":
-                if args[0] < G - 1:
-                    add_imag(args[0], args[1], slice(0, 512), banks["B", args[0], args[1]][:])
-                else:
-                    add_imag_half(args[0], args[1] // 2, args[1] % 2)
-            if name in ("pc", "ps", "sort", "Q", "IL", "QZ", "EB") or token[len(token) - 1 :] == "V":
-                vector_steps += 1
-                if vector_steps > 2 and trig:
-                    trig[0]()
-                    trig = trig[1:]
+        def turn_run(c, part, on_vector):
+            for i in range(4):
+                turn(c, part, i)
+                turn_out(c, part, i, i in on_vector)
+
+        def real_run(c):
+            for t in range(4):
+                banks["A", c, t] = project(c, 0, t)
+                real_out(c, t)
+
+        def imag_run(c):
+            for t in range(4):
+                banks["B", c, t] = project(c, 1, t)
+                add_imag(c, t, slice(0, 512), banks["B", c, t][:])
+
+        def expand_row(c, i, on_vector):
+            for n in range(2):
+                expand(c, i, n)
+                expand_out(c, i, n, n in on_vector)
+
+        def quantize_rows(c):
+            for i in range(0, 4, 2):
+                interleave(c, i)
+                interleave(c, i + 1)
+                quantize_z(c, i)
+                quantize_z(c, i + 1)
+
+        turn_run(0, 0, (1,))
+        trig_turns()
+        quantize(0, 0, 0, 0, 2)
+        trig_reduce()
+        quantize(0, 0, 1, 0, 2)
+        trig_wrap()
+        permute_group(0, 0)
+        permute_group(0, 1)
+        quantize(0, 0, 0, 2, 4)
+        quantize(0, 0, 1, 2, 4)
+        permute_scales(0)
+        turn_run(0, 1, ())
+        trig_sin()
+        permute_scales(1)
+        real_run(0)
+        quantize(0, 1, 0)
+        quantize(0, 1, 1)
+        permute_group(1, 0)
+        permute_group(1, 1)
+        turn_run(1, 0, (1, 3))
+        imag_run(0)
+        quantize(1, 0, 0)
+        quantize(1, 0, 1)
+
+        for c in range(3):
+            turn_run(c + 1, 1, ())
+            if c < 2:
+                permute_group(c + 2, 0)
+            quantize_rows(c)
+            quantize(c + 1, 1, 0)
+            quantize(c + 1, 1, 1)
+            real_run(c + 1)
+            if c < 2:
+                permute_group(c + 2, 1)
+                permute_scales(c + 2)
+                turn_run(c + 2, 0, (3,))
+                expand_row(c, 0, ())
+                expand_row(c, 1, (0,))
+                expand_row(c, 2, (0,))
+                expand_row(c, 3, ())
+                quantize(c + 2, 0, 0)
+                quantize(c + 2, 0, 1)
+                imag_run(c + 1)
+
+        expand_row(2, 0, (0,))
+        expand_row(2, 1, (0,))
+        for j in range(2):
+            imag_half(3, 0, j)
+            add_imag_half(3, 0, j)
+        expand_row(2, 2, (1,))
+        expand_row(2, 3, ())
+        interleave(3, 0)
+        interleave(3, 1)
+        quantize_z(3, 0)
+        for j in range(2):
+            imag_half(3, 1, j)
+            add_imag_half(3, 1, j)
+        quantize_z(3, 1)
+        interleave(3, 2)
+        interleave(3, 3)
+        quantize_z(3, 2)
+        quantize_z(3, 3)
+        for i in range(4):
+            expand_row(3, i, (1,) if i > 0 else ())

@@ -36,18 +36,18 @@ def tile_split_real_schrodinger_step_s14_kernel(tc, re, im, phase, v_words, v_sc
         vperm = []
         u = []
         for c in range(G):
-            t0 = keep.tile([P, 2, 1024], U8, name="vraw%d" % c, align_bytes=64)
-            t1 = keep.tile([P, 2, 4, 256], U8, name="vperm%d" % c, align_bytes=64)
-            t2 = keep.tile([P, 2048], U8, name="u%d" % c, align_bytes=64)
+            t0 = keep.tile([P, 2, 1024], U8, name="vraw%d" % c, align_bytes=256)
+            t1 = keep.tile([P, 2, 4, 256], U8, name="vperm%d" % c, align_bytes=256)
+            t2 = keep.tile([P, 2048], U8, name="u%d" % c, align_bytes=256)
             vraw.append(t0)
             vperm.append(t1)
             u.append(t2)
-        sraw = keep.tile([P, 8, 512], U8, name="sraw", align_bytes=64)
+        sraw = keep.tile([P, 8, 512], U8, name="sraw", align_bytes=256)
         sperm = []
         for c in range(G):
-            t3 = keep.tile([P, 2, 4, 128], U8, name="sperm%d" % c, align_bytes=64)
+            t3 = keep.tile([P, 2, 4, 128], U8, name="sperm%d" % c, align_bytes=256)
             sperm.append(t3)
-        us = keep.tile([P, 4, 1024], U8, name="us", align_bytes=64)
+        us = keep.tile([P, 4, 1024], U8, name="us", align_bytes=256)
         ident = keep.tile([P, P], F32, name="ident")
         ph = keep.tile([P, G, 4], BF16, name="ph")
         turns = keep.tile([P, G * 4], I32, name="turns")
@@ -71,8 +71,9 @@ def tile_split_real_schrodinger_step_s14_kernel(tc, re, im, phase, v_words, v_sc
         def load_u(c):
             nc.sync.dma_start(out=u[c][:].bitcast(I32), in_=u_words[c].bitcast(I32))
 
-        nc.vector.memset(sraw[:].bitcast(I32), 0)
+        nc.scalar.dma_start(out=ph[:], in_=phase.rearrange("c (p t) -> p c t", t=4))
         nc.vector.memset(dummy[:], 0.0)
+        nc.vector.memset(sraw[:].bitcast(I32), 0)
         nc.scalar.activation(out=dummy[:], in_=dummy[:], func=ACT.Sin)
         make_identity(nc, ident[:])
         nc.gpsimd.memset(us[:].bitcast(I32), 0)
@@ -81,14 +82,13 @@ def tile_split_real_schrodinger_step_s14_kernel(tc, re, im, phase, v_words, v_sc
         load_rows(0, 0, 1, 2)
         load_rows(0, 0, 2, 4)
         load_v(0)
-        nc.scalar.dma_start(out=ph[:], in_=phase.rearrange("c (p t) -> p c t", t=4))
-        load_rows(0, 1, 0, 2)
-        load_rows(0, 1, 2, 4)
         for q in range(4):
             nc.sync.dma_start(
                 out=sraw[:].bitcast(I32)[32 * q : 32 * q + 4, :, :],
                 in_=v_scales.bitcast(I32)[:, 4 * q : 4 * q + 4, :].rearrange("g r n -> r g n"),
             )
+        load_rows(0, 1, 0, 2)
+        load_rows(0, 1, 2, 4)
         load_all(1, 0)
         load_v(1)
         load_all(1, 1)
@@ -136,9 +136,9 @@ def tile_split_real_schrodinger_step_s14_kernel(tc, re, im, phase, v_words, v_sc
         scales = {}
 
         def new_unit(c, part):
-            gt = work.tile([P, 2, 2048], BF16, name="grouped", bufs=4, align_bytes=64)
-            ct = work.tile([P, 2, 512], U32, name="codes", bufs=4, align_bytes=64)
-            st = work.tile([P, 2, 512], U8, name="scales", bufs=4, align_bytes=64)
+            gt = work.tile([P, 2, 2048], BF16, name="grouped", bufs=4, align_bytes=256)
+            ct = work.tile([P, 2, 512], U32, name="codes", bufs=4, align_bytes=256)
+            st = work.tile([P, 2, 512], U8, name="scales", bufs=4, align_bytes=256)
             grouped[c, part] = gt
             codes[c, part] = ct
             scales[c, part] = st
@@ -146,7 +146,7 @@ def tile_split_real_schrodinger_step_s14_kernel(tc, re, im, phase, v_words, v_sc
         sorted_words = {}
 
         def sort_words(c, part, i):
-            w = work.tile([P, 512], F32, name="sorted_words", bufs=3)
+            w = work.tile([P, 512], F32, name="sorted_words", bufs=4)
             sorted_words[c, part, i] = w
             nc.vector.tensor_copy(
                 out=w[:].rearrange("p (g u r) -> p g u r", g=2, u=2),
@@ -229,9 +229,9 @@ def tile_split_real_schrodinger_step_s14_kernel(tc, re, im, phase, v_words, v_sc
 
         def new_z(c):
             z0 = work.tile([P, 4, 512], BF16, name="zrows", bufs=2)
-            z1 = work.tile([P, 512, 4], BF16, name="zgroup", bufs=2, align_bytes=64)
-            z2 = work.tile([P, 512], U32, name="zcodes", bufs=2, align_bytes=64)
-            z3 = work.tile([P, 512], U8, name="zscales", bufs=2, align_bytes=64)
+            z1 = work.tile([P, 512, 4], BF16, name="zgroup", bufs=2, align_bytes=256)
+            z2 = work.tile([P, 512], U32, name="zcodes", bufs=2, align_bytes=256)
+            z3 = work.tile([P, 512], U8, name="zscales", bufs=2, align_bytes=256)
             zrows[c] = z0
             zgroup[c] = z1
             zcodes[c] = z2
@@ -268,12 +268,37 @@ def tile_split_real_schrodinger_step_s14_kernel(tc, re, im, phase, v_words, v_sc
             for k in range(2):
                 add_imag(c, 2 * j + k, slice(256 * h, 256 * (h + 1)), b[:, 256 * k : 256 * (k + 1)])
 
-        def interleave(c, i):
+        def project_row(c, i):
+            b = bank()
             cols = slice(128 * i, 128 * (i + 1))
-            nc.vector.tensor_copy(out=zgroup[c][:, cols, :], in_=zrows[c][:, :, cols].rearrange("p t n -> p n t"))
+            for t in range(4):
+                for g in range(2):
+                    nc.tensor.matmul_mx(
+                        out=b[:, 128 * t : 128 * (t + 1)],
+                        lhsT=vperm[c][:, g, t, :].bitcast(FP4X4),
+                        lhsT_scale=sperm[c][:, g, t, :],
+                        rhs=codes[c, 1][:, g, cols].bitcast(FP8X4),
+                        rhs_scale=scales[c, 1][:, g, cols],
+                        start=(g == 0),
+                        stop=(g == 1),
+                    )
+            return b
 
-        def quantize_z(c, i):
-            cols = slice(128 * i, 128 * (i + 1))
+        def add_imag_row(c, i, b):
+            for t in range(4):
+                add_imag(c, t, slice(128 * i, 128 * (i + 1)), b[:, 128 * t : 128 * (t + 1)])
+
+        def interleave(c, i, j, on_scalar=False):
+            cols = slice(128 * i, 128 * j)
+            dst = zgroup[c][:, cols, :]
+            source = zrows[c][:, :, cols].rearrange("p t n -> p n t")
+            if on_scalar:
+                nc.scalar.copy(out=dst, in_=source)
+            else:
+                nc.vector.tensor_copy(out=dst, in_=source)
+
+        def quantize_z(c, i, j):
+            cols = slice(128 * i, 128 * j)
             nc.vector.quantize_mx(
                 out=zcodes[c][:, cols].bitcast(FP8X4), scales=zscales[c][:, cols],
                 in_=zgroup[c][:, cols, :].rearrange("p n t -> p (n t)"),
@@ -302,7 +327,7 @@ def tile_split_real_schrodinger_step_s14_kernel(tc, re, im, phase, v_words, v_sc
                 out_rows[c, i] = o
             cols = slice(512 * n, 512 * (n + 1))
             copy_out(out_rows[c, i][:, cols], banks["O", c, i, n][:], on_vector)
-            if c == 3:
+            if c == 3 and i == 3:
                 nc.sync.dma_start(out=out[c].rearrange("(p i) n -> p i n", i=4)[:, i, cols], in_=out_rows[c, i][:, cols])
             elif second:
                 nc.sync.dma_start(out=out[c].rearrange("(p i) n -> p i n", i=4)[:, i, :], in_=out_rows[c, i][:])
@@ -328,19 +353,30 @@ def tile_split_real_schrodinger_step_s14_kernel(tc, re, im, phase, v_words, v_sc
                 expand_out(c, i, n, n in on_vector)
 
         def quantize_rows(c):
-            for i in range(0, 4, 2):
-                interleave(c, i)
-                interleave(c, i + 1)
-                quantize_z(c, i)
-                quantize_z(c, i + 1)
+            interleave(c, 0, 2)
+            interleave(c, 2, 4)
+            quantize_z(c, 0, 2)
+            quantize_z(c, 2, 4)
 
-        turn_run(0, 0, (1,))
-        trig_turns()
-        quantize(0, 0, 0, 0, 2)
-        trig_reduce()
-        quantize(0, 0, 1, 0, 2)
+        def quantize_all(c, part):
+            nc.vector.quantize_mx(
+                out=codes[c, part][:].rearrange("p g n -> p (g n)").bitcast(FP8X4),
+                scales=scales[c, part][:].rearrange("p g n -> p (g n)"),
+                in_=grouped[c, part][:].rearrange("p g n -> p (g n)"),
+            )
+
+        for i in range(4):
+            sort_words(0, 0, i)
+            turn(0, 0, i)
+            turn_out(0, 0, i, False)
+            if i == 1:
+                trig_turns()
+            if i == 2:
+                trig_reduce()
         trig_wrap()
         permute_group(0, 0)
+        quantize(0, 0, 0, 0, 2)
+        quantize(0, 0, 1, 0, 2)
         permute_group(0, 1)
         quantize(0, 0, 0, 2, 4)
         quantize(0, 0, 1, 2, 4)
@@ -349,22 +385,19 @@ def tile_split_real_schrodinger_step_s14_kernel(tc, re, im, phase, v_words, v_sc
         trig_sin()
         permute_scales(1)
         real_run(0)
-        quantize(0, 1, 0)
-        quantize(0, 1, 1)
+        quantize_all(0, 1)
         permute_group(1, 0)
         permute_group(1, 1)
         turn_run(1, 0, (1, 3))
         imag_run(0)
-        quantize(1, 0, 0)
-        quantize(1, 0, 1)
+        quantize_all(1, 0)
 
         for c in range(3):
             turn_run(c + 1, 1, ())
             if c < 2:
                 permute_group(c + 2, 0)
             quantize_rows(c)
-            quantize(c + 1, 1, 0)
-            quantize(c + 1, 1, 1)
+            quantize_all(c + 1, 1)
             real_run(c + 1)
             if c < 2:
                 permute_group(c + 2, 1)
@@ -374,8 +407,7 @@ def tile_split_real_schrodinger_step_s14_kernel(tc, re, im, phase, v_words, v_sc
                 expand_row(c, 1, (0,))
                 expand_row(c, 2, (0,))
                 expand_row(c, 3, ())
-                quantize(c + 2, 0, 0)
-                quantize(c + 2, 0, 1)
+                quantize_all(c + 2, 0)
                 imag_run(c + 1)
 
         expand_row(2, 0, (0,))
@@ -383,18 +415,21 @@ def tile_split_real_schrodinger_step_s14_kernel(tc, re, im, phase, v_words, v_sc
         for j in range(2):
             imag_half(3, 0, j)
             add_imag_half(3, 0, j)
-        expand_row(2, 2, (1,))
+        expand_row(2, 2, ())
+        interleave(3, 0, 1)
+        interleave(3, 1, 2)
+        quantize_z(3, 0, 1)
+        b2 = project_row(3, 2)
+        add_imag_row(3, 2, b2)
+        quantize_z(3, 1, 2)
         expand_row(2, 3, ())
-        interleave(3, 0)
-        interleave(3, 1)
-        quantize_z(3, 0)
-        for j in range(2):
-            imag_half(3, 1, j)
-            add_imag_half(3, 1, j)
-        quantize_z(3, 1)
-        interleave(3, 2)
-        interleave(3, 3)
-        quantize_z(3, 2)
-        quantize_z(3, 3)
-        for i in range(4):
-            expand_row(3, i, (1,) if i > 0 else ())
+        b3 = project_row(3, 3)
+        interleave(3, 2, 3)
+        add_imag_row(3, 3, b3)
+        quantize_z(3, 2, 3)
+        expand_row(3, 0, ())
+        interleave(3, 3, 4)
+        expand_row(3, 1, ())
+        quantize_z(3, 3, 4)
+        expand_row(3, 2, (1,))
+        expand_row(3, 3, (1,))

from contextlib import ExitStack
import math

import concourse.mybir as mybir
from concourse.masks import make_identity

G, M, K, F, N = 4, 512, 1024, 512, 1024
FLOPS = 2 * G * (2 * M * K * F + M * F * N)

F32 = mybir.dt.float32
BF16 = mybir.dt.bfloat16
U32 = mybir.dt.uint32
I32 = mybir.dt.int32
U8 = mybir.dt.uint8
FP8X4 = mybir.dt.float8_e4m3fn_x4
FP4X4 = mybir.dt.float4_e2m1fn_x4
ALU = mybir.AluOpType
ACT = mybir.ActivationFunctionType
P = 128


def tile_split_real_schrodinger_step_s14_kernel(tc, re, im, phase, v_words, v_scales, u_words, u_scales, out):
    nc = tc.nc
    with ExitStack() as ctx:
        keep = ctx.enter_context(tc.tile_pool(name="keep", bufs=1))
        work = ctx.enter_context(tc.tile_pool(name="work", bufs=3))
        psum = ctx.enter_context(tc.psum_pool(name="psum", bufs=8))
        ctx.enter_context(tc.manual_schedule())

        x = {}
        for c in range(G):
            for part in range(2):
                xt = keep.tile([P, 4, K], BF16, name="x%d_%d" % (c, part))
                x[c, part] = xt
        vraw = []
        vperm = []
        u = []
        for c in range(G):
            t0 = keep.tile([P, 2, 1024], U8, name="vraw%d" % c, align_bytes=256)
            t1 = keep.tile([P, 2, 4, 256], U8, name="vperm%d" % c, align_bytes=256)
            t2 = keep.tile([P, 2048], U8, name="u%d" % c, align_bytes=256)
            vraw.append(t0)
            vperm.append(t1)
            u.append(t2)
        sraw = keep.tile([P, 8, 512], U8, name="sraw", align_bytes=256)
        sperm = []
        for c in range(G):
            t3 = keep.tile([P, 2, 4, 128], U8, name="sperm%d" % c, align_bytes=256)
            sperm.append(t3)
        us = keep.tile([P, 4, 1024], U8, name="us", align_bytes=256)
        ident = keep.tile([P, P], F32, name="ident")
        ph = keep.tile([P, G, 4], BF16, name="ph")
        turns = keep.tile([P, G * 4], I32, name="turns")
        arg = keep.tile([P, 2, G * 4], F32, name="arg")
        high = keep.tile([P, 2, G * 4], F32, name="high")
        low = keep.tile([P, 2, G * 4], F32, name="low")
        sc = keep.tile([P, 2, G * 4], F32, name="sc")
        dummy = keep.tile([P, 1], F32, name="dummy")

        src = (re, im)

        def load_rows(c, part, i0, i1):
            nc.sync.dma_start(out=x[c, part][:, i0:i1, :], in_=src[part][c].rearrange("(p i) k -> p i k", i=4)[:, i0:i1, :])

        def load_all(c, part):
            load_rows(c, part, 0, 4)

        def load_v(c):
            nc.sync.dma_start(out=vraw[c][:].bitcast(I32), in_=v_words[2 * c : 2 * c + 2].bitcast(I32).rearrange("g p b -> p g b"))

        def load_u(c):
            nc.sync.dma_start(out=u[c][:].bitcast(I32), in_=u_words[c].bitcast(I32))

        nc.scalar.dma_start(out=ph[:], in_=phase.rearrange("c (p t) -> p c t", t=4))
        nc.vector.memset(dummy[:], 0.0)
        nc.vector.memset(sraw[:].bitcast(I32), 0)
        nc.scalar.activation(out=dummy[:], in_=dummy[:], func=ACT.Sin)
        make_identity(nc, ident[:])
        nc.gpsimd.memset(us[:].bitcast(I32), 0)

        load_rows(0, 0, 0, 1)
        load_rows(0, 0, 1, 2)
        load_rows(0, 0, 2, 4)
        load_v(0)
        for q in range(4):
            nc.sync.dma_start(
                out=sraw[:].bitcast(I32)[32 * q : 32 * q + 4, :, :],
                in_=v_scales.bitcast(I32)[:, 4 * q : 4 * q + 4, :].rearrange("g r n -> r g n"),
            )
        load_rows(0, 1, 0, 2)
        load_rows(0, 1, 2, 4)
        load_all(1, 0)
        load_v(1)
        load_all(1, 1)
        load_u(0)
        for q in range(4):
            nc.sync.dma_start(
                out=us[:].bitcast(I32)[32 * q : 32 * q + 4, :, :],
                in_=u_scales.bitcast(I32)[:, 4 * q : 4 * q + 4, :].rearrange("c r n -> r c n"),
            )
        load_all(2, 0)
        load_v(2)
        load_all(2, 1)
        load_u(1)
        load_all(3, 0)
        load_v(3)
        load_all(3, 1)
        load_u(2)
        load_u(3)

        phf = ph[:].rearrange("p c t -> p (c t)")
        angle = arg[:, 0, :]

        def trig_turns():
            nc.vector.tensor_scalar(out=turns[:], in0=phf, scalar1=1.0 / (2.0 * math.pi), scalar2=None, op0=ALU.mult)

        def trig_reduce():
            nc.vector.scalar_tensor_tensor(out=angle, in0=turns[:], scalar=-2.0 * math.pi, in1=phf, op0=ALU.mult, op1=ALU.add)

        def trig_wrap():
            nc.gpsimd.tensor_scalar(out=arg[:, 1, :], in0=angle, scalar1=1.0, scalar2=0.5 * math.pi, op0=ALU.mult, op1=ALU.add)
            nc.gpsimd.tensor_scalar(out=high[:], in0=arg[:], scalar1=math.pi, scalar2=-2.0 * math.pi, op0=ALU.is_gt, op1=ALU.mult)
            nc.gpsimd.tensor_scalar(out=low[:], in0=arg[:], scalar1=-math.pi, scalar2=2.0 * math.pi, op0=ALU.is_lt, op1=ALU.mult)
            nc.gpsimd.tensor_tensor(out=arg[:], in0=arg[:], in1=high[:], op=ALU.add)
            nc.gpsimd.tensor_tensor(out=arg[:], in0=arg[:], in1=low[:], op=ALU.add)

        def trig_sin():
            nc.scalar.activation(out=sc[:], in_=arg[:], func=ACT.Sin)

        def bank():
            b = psum.tile([P, 512], F32, name="bank")
            return b

        grouped = {}
        codes = {}
        scales = {}

        def new_unit(c, part):
            gt = work.tile([P, 2, 2048], BF16, name="grouped", bufs=4, align_bytes=256)
            ct = work.tile([P, 2, 512], U32, name="codes", bufs=4, align_bytes=256)
            st = work.tile([P, 2, 512], U8, name="scales", bufs=4, align_bytes=256)
            grouped[c, part] = gt
            codes[c, part] = ct
            scales[c, part] = st

        sorted_words = {}

        def sort_words(c, part, i):
            w = work.tile([P, 512], F32, name="sorted_words", bufs=4)
            sorted_words[c, part, i] = w
            nc.vector.tensor_copy(
                out=w[:].rearrange("p (g u r) -> p g u r", g=2, u=2),
                in_=x[c, part][:].bitcast(F32)[:, i, :].rearrange("p (g r u) -> p g u r", g=2, u=2),
            )

        banks = {}

        def turn(c, part, i):
            words = x[c, part][:].bitcast(F32)
            b = bank()
            banks["T", c, part, i] = b
            bv = b[:].rearrange("p (g u r) -> p g u r", g=2, u=2)
            for g in range(2):
                for e in range(2):
                    if (c, part, i) in sorted_words:
                        w0 = 256 * g + 128 * e
                        source = sorted_words[c, part, i][:, w0 : w0 + 128]
                    else:
                        source = words[:, i, 256 * g + e : 256 * (g + 1) : 2]
                    nc.tensor.transpose(bv[:, g, e, :], source, ident[:])

        def copy_out(dst, s, on_vector):
            if on_vector:
                nc.vector.tensor_copy(out=dst, in_=s)
            else:
                nc.scalar.copy(out=dst, in_=s)

        def turn_out(c, part, i, on_vector):
            if (c, part) not in grouped:
                new_unit(c, part)
            dst = grouped[c, part][:].bitcast(F32).rearrange("p g (n u) -> p g n u", u=2)[:, :, 128 * i : 128 * (i + 1), :]
            copy_out(dst, banks["T", c, part, i][:].rearrange("p (g u r) -> p g r u", g=2, u=2), on_vector)

        def quantize(c, part, g, i0=0, i1=4):
            cols = slice(128 * i0, 128 * i1)
            nc.vector.quantize_mx(
                out=codes[c, part][:, g, cols].bitcast(FP8X4), scales=scales[c, part][:, g, cols],
                in_=grouped[c, part][:, g, 512 * i0 : 512 * i1],
            )

        def permute_codes(c):
            for g in range(2):
                permute_group(c, g)

        def permute_group(c, g):
            if True:
                nc.vector.tensor_copy(
                    out=vperm[c][:, g, :, :].rearrange("p t (m b) -> p t m b", b=2),
                    in_=vraw[c][:, g, :].rearrange("p (m t b) -> p t m b", t=4, b=2),
                )

        def permute_scales(c):
            nc.vector.tensor_copy(out=sperm[c][:], in_=sraw[:, 2 * c : 2 * c + 2, :].rearrange("p g (m t) -> p g t m", t=4))

        def project(c, part, t):
            b = bank()
            for g in range(2):
                nc.tensor.matmul_mx(
                    out=b[:],
                    lhsT=vperm[c][:, g, t, :].bitcast(FP4X4),
                    lhsT_scale=sperm[c][:, g, t, :],
                    rhs=codes[c, part][:, g, :].bitcast(FP8X4),
                    rhs_scale=scales[c, part][:, g, :],
                    start=(g == 0),
                    stop=(g == 1),
                )
            return b

        acos = {}
        zrows = {}
        zgroup = {}
        zcodes = {}
        zscales = {}

        def real_out(c, t):
            a = work.tile([P, 512], F32, name="acos", bufs=6)
            acos[c, t] = a
            nc.scalar.activation(out=a[:], in_=banks["A", c, t][:], func=ACT.Copy, scale=sc[:, 1, 4 * c + t : 4 * c + t + 1])

        def new_z(c):
            z0 = work.tile([P, 4, 512], BF16, name="zrows", bufs=2)
            z1 = work.tile([P, 512, 4], BF16, name="zgroup", bufs=2, align_bytes=256)
            z2 = work.tile([P, 512], U32, name="zcodes", bufs=2, align_bytes=256)
            z3 = work.tile([P, 512], U8, name="zscales", bufs=2, align_bytes=256)
            zrows[c] = z0
            zgroup[c] = z1
            zcodes[c] = z2
            zscales[c] = z3

        def add_imag(c, t, cols, b):
            if c not in zrows:
                new_z(c)
            nc.vector.scalar_tensor_tensor(
                out=zrows[c][:, t, cols], in0=b, scalar=sc[:, 0, 4 * c + t : 4 * c + t + 1], in1=acos[c, t][:, cols],
                op0=ALU.mult, op1=ALU.add,
            )

        def imag_half(c, h, j):
            b = bank()
            banks["B", c, 2 * h + j] = b
            for k in range(2):
                t = 2 * j + k
                for r in range(2):
                    cols = slice(256 * h + 128 * r, 256 * h + 128 * (r + 1))
                    for g in range(2):
                        nc.tensor.matmul_mx(
                            out=b[:, 256 * k + 128 * r : 256 * k + 128 * (r + 1)],
                            lhsT=vperm[c][:, g, t, :].bitcast(FP4X4),
                            lhsT_scale=sperm[c][:, g, t, :],
                            rhs=codes[c, 1][:, g, cols].bitcast(FP8X4),
                            rhs_scale=scales[c, 1][:, g, cols],
                            start=(g == 0),
                            stop=(g == 1),
                        )

        def add_imag_half(c, h, j):
            b = banks["B", c, 2 * h + j]
            for k in range(2):
                add_imag(c, 2 * j + k, slice(256 * h, 256 * (h + 1)), b[:, 256 * k : 256 * (k + 1)])

        def project_row(c, i):
            b = bank()
            cols = slice(128 * i, 128 * (i + 1))
            for t in range(4):
                for g in range(2):
                    nc.tensor.matmul_mx(
                        out=b[:, 128 * t : 128 * (t + 1)],
                        lhsT=vperm[c][:, g, t, :].bitcast(FP4X4),
                        lhsT_scale=sperm[c][:, g, t, :],
                        rhs=codes[c, 1][:, g, cols].bitcast(FP8X4),
                        rhs_scale=scales[c, 1][:, g, cols],
                        start=(g == 0),
                        stop=(g == 1),
                    )
            return b

        def add_imag_row(c, i, b):
            for t in range(4):
                add_imag(c, t, slice(128 * i, 128 * (i + 1)), b[:, 128 * t : 128 * (t + 1)])

        def interleave(c, i, j, on_scalar=False):
            cols = slice(128 * i, 128 * j)
            dst = zgroup[c][:, cols, :]
            source = zrows[c][:, :, cols].rearrange("p t n -> p n t")
            if on_scalar:
                nc.scalar.copy(out=dst, in_=source)
            else:
                nc.vector.tensor_copy(out=dst, in_=source)

        def quantize_z(c, i, j):
            cols = slice(128 * i, 128 * j)
            nc.vector.quantize_mx(
                out=zcodes[c][:, cols].bitcast(FP8X4), scales=zscales[c][:, cols],
                in_=zgroup[c][:, cols, :].rearrange("p n t -> p (n t)"),
            )

        out_rows = {}

        def expand(c, i, n):
            cols = slice(128 * i, 128 * (i + 1))
            b = bank()
            banks["O", c, i, n] = b
            nc.tensor.matmul_mx(
                out=b[:],
                lhsT=zcodes[c][:, cols].bitcast(FP8X4),
                lhsT_scale=zscales[c][:, cols],
                rhs=u[c][:, 1024 * n : 1024 * (n + 1)].bitcast(FP4X4),
                rhs_scale=us[:, c, 512 * n : 512 * (n + 1)],
                start=True,
                stop=True,
            )

        def expand_out(c, i, n, on_vector):
            second = (c, i) in out_rows
            if not second:
                o = work.tile([P, 1024], F32, name="orow", bufs=8)
                out_rows[c, i] = o
            cols = slice(512 * n, 512 * (n + 1))
            copy_out(out_rows[c, i][:, cols], banks["O", c, i, n][:], on_vector)
            if c == 3 and i == 3:
                nc.sync.dma_start(out=out[c].rearrange("(p i) n -> p i n", i=4)[:, i, cols], in_=out_rows[c, i][:, cols])
            elif second:
                nc.sync.dma_start(out=out[c].rearrange("(p i) n -> p i n", i=4)[:, i, :], in_=out_rows[c, i][:])

        def turn_run(c, part, on_vector):
            for i in range(4):
                turn(c, part, i)
                turn_out(c, part, i, i in on_vector)

        def real_run(c):
            for t in range(4):
                banks["A", c, t] = project(c, 0, t)
                real_out(c, t)

        def imag_run(c):
            for t in range(4):
                banks["B", c, t] = project(c, 1, t)
                add_imag(c, t, slice(0, 512), banks["B", c, t][:])

        def expand_row(c, i, on_vector):
            for n in range(2):
                expand(c, i, n)
                expand_out(c, i, n, n in on_vector)

        def quantize_rows(c):
            interleave(c, 0, 2)
            interleave(c, 2, 4)
            quantize_z(c, 0, 2)
            quantize_z(c, 2, 4)

        def quantize_all(c, part):
            nc.vector.quantize_mx(
                out=codes[c, part][:].rearrange("p g n -> p (g n)").bitcast(FP8X4),
                scales=scales[c, part][:].rearrange("p g n -> p (g n)"),
                in_=grouped[c, part][:].rearrange("p g n -> p (g n)"),
            )

        for i in range(4):
            sort_words(0, 0, i)
            turn(0, 0, i)
            turn_out(0, 0, i, False)
            if i == 1:
                trig_turns()
            if i == 2:
                trig_reduce()
        trig_wrap()
        permute_group(0, 0)
        quantize(0, 0, 0, 0, 2)
        quantize(0, 0, 1, 0, 2)
        permute_group(0, 1)
        quantize(0, 0, 0, 2, 4)
        quantize(0, 0, 1, 2, 4)
        permute_scales(0)
        turn_run(0, 1, ())
        trig_sin()
        permute_scales(1)
        real_run(0)
        quantize_all(0, 1)
        permute_group(1, 0)
        permute_group(1, 1)
        turn_run(1, 0, (1, 3))
        imag_run(0)
        quantize_all(1, 0)

        for c in range(3):
            turn_run(c + 1, 1, ())
            if c < 2:
                permute_group(c + 2, 0)
            quantize_rows(c)
            quantize_all(c + 1, 1)
            real_run(c + 1)
            if c < 2:
                permute_group(c + 2, 1)
                permute_scales(c + 2)
                turn_run(c + 2, 0, (3,))
                expand_row(c, 0, ())
                expand_row(c, 1, (0,))
                expand_row(c, 2, (0,))
                expand_row(c, 3, ())
                quantize_all(c + 2, 0)
                imag_run(c + 1)

        expand_row(2, 0, (0,))
        expand_row(2, 1, (0,))
        for j in range(2):
            imag_half(3, 0, j)
            add_imag_half(3, 0, j)
        expand_row(2, 2, ())
        interleave(3, 0, 1)
        interleave(3, 1, 2)
        quantize_z(3, 0, 1)
        b2 = project_row(3, 2)
        add_imag_row(3, 2, b2)
        quantize_z(3, 1, 2)
        expand_row(2, 3, ())
        b3 = project_row(3, 3)
        interleave(3, 2, 3)
        add_imag_row(3, 3, b3)
        quantize_z(3, 2, 3)
        expand_row(3, 0, ())
        interleave(3, 3, 4)
        expand_row(3, 1, ())
        quantize_z(3, 3, 4)
        expand_row(3, 2, (1,))
        expand_row(3, 3, (1,))
